import numpy as np, ml_dtypes
CORES = [2,3,42,43,82,83,122,123]
N = 8
import mx_ref
BF = ml_dtypes.bfloat16
def entries(a):
    return np.ascontiguousarray(a.T).reshape(-1)
def table(e):
    return np.ascontiguousarray(np.reshape(e, (-1, 16)).T).astype(np.int32)
def cols(t, e):
    v = np.concatenate([t.reshape(128, -1, 4), np.zeros((128, 1, 4), BF)], axis=1)
    return np.ascontiguousarray(v[:, e]).reshape(128, -1)
def f(rng, *shape):
    return mx_ref.flush((rng.standard_normal(shape, dtype=np.float32) * np.exp2(rng.integers(-2, 3, shape[:-1] + (1,)))).astype(BF))
def wide(rng, *shape, cols=0):
    v = rng.standard_normal(shape, dtype=np.float32) * np.exp2(rng.integers(-12, 13, shape)).astype(np.float32)
    if cols: v *= np.repeat(np.exp2(rng.integers(-cols, cols + 1, shape[:-2] + (1, shape[-1] // 4))) * (rng.random(shape[:-2] + (1, shape[-1] // 4)) > 0.0625), 4, axis=-1).astype(np.float32)
    return mx_ref.flush(v.astype(BF))
T, CAPP = 512, 96
def lists(rng, full=False, skew=False, single=False, back=False):
    if full:
        v = rng.permutation(([CAPP] * (T // CAPP) + [T % CAPP] + [0] * N)[:N])
        n = v[(np.arange(N)[None, :] - np.arange(N)[:, None]) % N][rng.permutation(N)][:, rng.permutation(N)]
    else:
        n = np.full((N, N), T // N)
        for _ in range(20 * N):
            (s, t), (d, e) = rng.permutation(N)[:2], rng.permutation(N)[:2]
            k = rng.integers(0, min(n[s, d], n[t, e], CAPP - n[s, e], CAPP - n[t, d]) + 1)
            n[s, d] -= k; n[t, e] -= k; n[s, e] += k; n[t, d] += k
    a = np.full((N, N * CAPP), -1)
    for s in range(N):
        parts = np.split(rng.permutation(T), np.cumsum(n[s])[:-1])
        for d in range(N): a[s, d * CAPP + rng.permutation(CAPP)[:n[s, d]]] = parts[d]
    p, u, o = [], [], []
    for r in range(N):
        used = np.flatnonzero(a[:, r * CAPP:(r + 1) * CAPP].reshape(-1) >= 0)
        p.append(table(used[::-1] if back else rng.permutation(used)))
        h = rng.integers(0, N)
        c = rng.integers(0, 2, N) if full else (np.full(N, -1) if rng.random() < 0.5 else rng.integers(0, 2, N)) if single else rng.integers(-1, 2, N)
        if c[h] < 0: c[h] = rng.integers(0, 2)
        named = np.flatnonzero(c >= 0)
        if single: named = np.array([h])
        if skew:
            m = rng.integers(T // 2 + 1, T + 1)
            e = np.sort(np.concatenate([np.full(m, h), rng.choice(named, T - m)]))
        elif full: e = np.sort(np.concatenate([named, rng.choice(named, T - N)]))
        else: e = np.repeat(named, np.diff(np.concatenate([[0], np.sort(rng.integers(0, T + 1, len(named) - 1)), [T]])))
        u.append(table(np.concatenate([c, np.full(16 - N, -1)]))); o.append(table(e))
    return {"send": np.stack([table(k) for k in a]), "place": np.stack(p), "sel": np.stack(u), "of": np.stack(o)}
def setup_inputs(rng):
    return {"x": f(rng, N, 128, 4 * T), "w": f(rng, N, 256, 512), **lists(rng)}
def setup_inputs_full(rng):
    return {**setup_inputs(rng), **lists(rng, full=True)}
def setup_inputs_reversed(rng):
    return {**setup_inputs(rng), **lists(rng, back=True)}
def setup_inputs_single(rng):
    return {**setup_inputs(rng), **lists(rng, single=True)}
def setup_inputs_skew(rng):
    return {**setup_inputs(rng), **lists(rng, skew=True)}
def setup_inputs_spread(rng):
    d = setup_inputs(rng); d["x"] = wide(rng, N, 128, 4 * T, cols=8); return d
def check_inputs(d):
    b = []
    for k in ("x", "w"):
        a = np.abs(d[k].astype(np.float32))
        if not ((a == 0) | ((a >= 2.0 ** -30) & (a <= 2.0 ** 30))).all(): b.append(k)
    sends = np.stack([entries(d["send"][r]) for r in range(N)])
    for r in range(N):
        c, p, u, e = sends[r], entries(d["place"][r]), entries(d["sel"][r]), entries(d["of"][r])
        if c.min() < -1 or not np.array_equal(np.sort(c[c >= 0]), np.arange(T)): b.append("send")
        if not np.array_equal(np.sort(p), np.flatnonzero(sends[:, r * CAPP:(r + 1) * CAPP].reshape(-1) >= 0)): b.append("place")
        if u.min() < -1 or u.max() > 1 or (u[N:] != -1).any(): b.append("sel")
        if e.min() < 0 or e.max() >= N or (np.diff(e) < 0).any() or (u[e] < 0).any(): b.append("of")
    return b
def reference(x, w, send, place, sel, of):
    W = [[mx_ref.quantize(w[h][128 * m:128 * m + 128]) for m in range(2)] for h in range(N)]
    y = np.zeros((N, 128, T), np.float32)
    for r in range(N):
        slots = np.concatenate([cols(x[s], entries(send[s])[r * CAPP:(r + 1) * CAPP]) for s in range(N)], axis=1)
        X = mx_ref.quantize(cols(slots, entries(place[r])))
        u, e = entries(sel[r]), entries(of[r])
        for h in range(N):
            i = e == h
            if i.any(): y[r][:, i] = mx_ref.matmul(W[h][u[h]], X)[:, i]
    return {"y": y}

@@ -1,0 +1,401 @@
+from concourse.bass import DstId, RemoteDMATransfer
+from concourse.mybir import dt, AluOpType, ActivationFunctionType
+
+N, CAPP, TK = 8, 96, 512
+NS = N * CAPP
+HALF = NS // 2
+SP = 40
+TORD = (1, 3, 2)
+EORD = (3, 2)
+SCRATCH = {
+    "xs": ("sbuf", [128, 4 * TK], "bfloat16"),
+    "ws": ("sbuf", [128, 1024], "bfloat16"),
+    "sendl": ("sbuf", [128, 48], "int32"),
+    "soff": ("sbuf", [128, 48], "uint16"),
+    "r_c": ("sbuf", [128, CAPP + NS], "float8_e4m3fn_x4"),
+    "r_s": ("sbuf", [128, CAPP + NS], "uint8"),
+    "w_c": ("sbuf", [128, 256], "float8_e4m3fn_x4"),
+    "w_s": ("sbuf", [128, 256], "uint8"),
+    "m_c": ("sbuf", [128, 256], "float8_e4m3fn_x4"),
+    "m_s": ("sbuf", [128, 256], "uint8"),
+    "u_c": ("sbuf", [128, 512], "float8_e4m3fn_x4"),
+    "u_s": ("sbuf", [128, 512], "uint8"),
+    "e_c": ("sbuf", [128, 512], "float8_e4m3fn_x4"),
+    "e_s": ("sbuf", [128, 512], "uint8"),
+    "xr_c": ("sbuf", [128, 256], "float8_e4m3fn_x4"),
+    "xr_s": ("sbuf", [128, 256], "uint8"),
+    "ia": ("sbuf", [128, 32], "int32"),
+    "ib": ("sbuf", [128, 32], "int32"),
+    "ic": ("sbuf", [128, 32], "int32"),
+    "lin": ("sbuf", [128, 32], "float32"),
+    "selo": ("sbuf", [1, 16], "int32"),
+    "self5": ("sbuf", [1, 16], "float32"),
+    "selb": ("sbuf", [128, 16], "float32"),
+    "sland": ("sbuf", [128, 4], "float32"),
+    "selk": ("sbuf", [16, 8], "float32"),
+    "plc": ("sbuf", [16, 32], "int32"),
+    "ofl": ("sbuf", [16, 32], "int32"),
+    "pu": ("sbuf", [16, 32], "uint16"),
+    "poff": ("sbuf", [128, 32], "uint16"),
+    "ps": ("psum", [128, 4096], "float32"),
+    "pw": ("sbuf", [128, 12 * NS], "float32"),
+    "yb": ("sbuf", [128, TK], "float32"),
+}
+for _k in range(14):
+    SCRATCH["f%d" % _k] = ("sbuf", [16, 32], "float32")
+for _k in range(4):
+    SCRATCH["tk%d" % _k] = ("sbuf", [128, 768], "bfloat16")
+for _k in range(1, 4):
+    SCRATCH["q%d_c" % _k] = ("sbuf", [128, 192], "float8_e4m3fn_x4")
+    SCRATCH["q%d_s" % _k] = ("sbuf", [128, 192], "uint8")
+for _k in (2, 3):
+    SCRATCH["et%d" % _k] = ("sbuf", [128, 1024], "bfloat16")
+    SCRATCH["eo%d" % _k] = ("sbuf", [128, 64], "uint16")
+    SCRATCH["x%d_c" % _k] = ("sbuf", [128, 256], "float8_e4m3fn_x4")
+    SCRATCH["x%d_s" % _k] = ("sbuf", [128, 256], "uint8")
+
+SEMAPHORES = (["srow", "lst", "xl", "wl", "pl", "iot", "ibs", "lns", "scs", "sbs", "sos", "wq", "sela", "sks", "sent",
+               "me", "un", "us", "tokM", "pr", "yg", "yh", "y0", "y1", "rec", "res", "evz"]
+              + ["fs%d" % k for k in range(5)] + ["tok%d" % k for k in range(1, 4)]
+              + ["%s%d" % (s, k) for k in range(4) for s in ("tq", "vg", "sg")]
+              + ["%s%d" % (s, k) for k in (2, 3) for s in ("eos", "vge", "sge", "eq", "rec", "res")]
+              + ["ex%d" % j for j in range(4)]
+              + ["mm%d" % i for i in range(24)] + ["ev%d" % i for i in range(16)])
+
+
+def _groups(cores, topo):
+    out = []
+    for q in range(len(cores)):
+        for grp in out:
+            if topo.chip(cores[grp[0]]) == topo.chip(cores[q]):
+                grp.append(q)
+                break
+        else:
+            out.append([q])
+    return out
+
+
+def _where(groups, q):
+    return [i for i in range(len(groups)) if q in groups[i]][0]
+
+
+def _relay(cores, groups, q, topo):
+    able = [c for c in topo.cores_of(cores[q]) if topo.die(c) != topo.die(cores[q]) and c not in cores
+            and all(topo.may_write(c, d) for d in cores)]
+    return able[groups[_where(groups, q)].index(q)]
+
+
+def _others(groups, q):
+    c, n = _where(groups, q), len(groups)
+    return [s for d in range(1, n) for s in groups[(c + d) % n]]
+
+
+def _base(groups, q):
+    c = _where(groups, q)
+    return (c - groups[c].index(q)) % len(groups)
+
+
+def _half_col(groups, q, hf):
+    second = groups[_where(groups, q)].index(q)
+    return hf * (HALF + CAPP) if second else CAPP + hf * HALF
+
+
+def _slot_col(groups, q, s):
+    c = _where(groups, s)
+    p = CAPP * (2 * ((c - _base(groups, q)) % len(groups)) + groups[c].index(s))
+    return _half_col(groups, q, p // HALF) + p % HALF
+
+
+def _write(g, T, topo, sent, es, to, d, s, sem):
+    ad = topo.addr(to)
+    g.remote_dma(d, s, sem, T.sem.sent, ad[1], ad[0], sum(1 << e for e in es))
+    sent[0] += len(es)
+
+
+def _pair(g, T, topo, sent, eng, trs):
+    half = len(eng) // 2
+    out = []
+    for i, (q, d, s, sem) in enumerate(trs):
+        ad = topo.addr(T.cores[q])
+        out.append(RemoteDMATransfer(dst_ids=[DstId(rid=ad[0], pnc=ad[1])], remote_sem=sem, srcs=[s], dsts=[d],
+                                     dma_engine_mask=sum(1 << e for e in eng[half * i:half * i + half])))
+    g.remote_dma_fused(out, local_sem=T.sem.sent)
+    sent[0] += 2 * half
+
+
+def _chosen(g, r, k, b, plane, groups, T, topo, sent, eng):
+    d = groups[(_where(groups, r) + k) % len(groups)][b]
+    j = _others(groups, d).index(r)
+    sem = T.sem["ex%d" % j]
+    if plane:
+        _write(g, T, topo, sent, eng, T.cores[d], T.e_s[:, 128 * j:128 * j + 128],
+               T["x%d_s" % k][:, 128 * b:128 * b + 128], sem)
+    else:
+        _write(g, T, topo, sent, eng, T.cores[d], T.e_c[:, 128 * j:128 * j + 128].bitcast(dt.uint8),
+               T["x%d_c" % k][:, 128 * b:128 * b + 128].bitcast(dt.uint8), sem)
+
+
+def _relay_program(g, core, r, groups, T, topo):
+    sent = [0]
+    eng = topo.engines(core, T.cores[_others(groups, r)[0]])
+    ups = [e for e in topo.engines(core, T.cores[r]) if e not in eng]
+    ci = _where(groups, r)
+    j = 128 * groups[ci].index(r)
+    to = groups[(ci + 1) % len(groups)]
+    g.wait_ge(T.sem.rec, len(ups))
+    _pair(g, T, topo, sent, eng, [(d, T.u_c[:, j:j + 128].bitcast(dt.uint8), T.xr_c[:, 128 * b:128 * b + 128].bitcast(dt.uint8),
+                                   T.sem.un) for b, d in enumerate(to)])
+    g.wait_ge(T.sem.res, len(ups))
+    _pair(g, T, topo, sent, eng, [(d, T.u_s[:, j:j + 128], T.xr_s[:, 128 * b:128 * b + 128], T.sem.un) for b, d in enumerate(to)])
+    for k in EORD:
+        g.wait_ge(T.sem["rec%d" % k], len(ups))
+        _chosen(g, r, k, 1, False, groups, T, topo, sent, eng)
+        g.wait_ge(T.sem["res%d" % k], len(ups))
+        _chosen(g, r, k, 1, True, groups, T, topo, sent, eng)
+    g.wait_ge(T.sem.sent, sent[0])
+
+
+def rank_program(g, core, T, topo):
+    cores = T.cores
+    groups = _groups(cores, topo)
+    C = len(groups)
+    r = T.rank_of(core)
+    if r is None:
+        for q in range(N):
+            if _relay(cores, groups, q, topo) == core:
+                _relay_program(g, core, q, groups, T, topo)
+        return
+
+    ci = _where(groups, r)
+    mine = groups[ci].index(r)
+    mate = [q for q in groups[ci] if q != r][0]
+    oth = _others(groups, r)
+    prev = groups[(ci - 1) % C]
+    rel = _relay(cores, groups, r, topo)
+    S = T.sem
+    V, A, Te, Y = g.vector, g.scalar, g.tensor, g.sync
+    Copy = ActivationFunctionType.Copy
+    U8 = dt.uint8
+    add, mul = AluOpType.add, AluOpType.mult
+    eng = topo.engines(core, cores[oth[0]])
+    ups = [e for e in topo.engines(core, cores[mate]) if e not in eng]
+    sent = [0]
+
+    def chip_write(to, d, s, sem):
+        _write(g, T, topo, sent, ups, to, d, s, sem)
+
+    Y.dma_start(T.selo[0:1, 0:16], T.sel[:, :]).then_inc(S.srow, 16)
+    A.dma_start(T.plc[:, :], T.place[:, :]).then_inc(S.pl, 16)
+    A.dma_start(T.ofl[:, :], T["of"][:, :]).then_inc(S.pl, 16)
+    for k in range(4):
+        Y.dma_start(T.sendl[16 * k:16 * k + 16, :], T.send[:, :]).then_inc(S.lst, 16)
+        A.dma_start(T.sendl[64 + 16 * k:80 + 16 * k, :], T.send[:, :]).then_inc(S.lst, 16)
+    for e in range(2):
+        Y.dma_start(T.ws[:, 512 * e:512 * e + 512], T.w[128 * e:128 * e + 128, :]).then_inc(S.wl, 16)
+    A.dma_start(T.xs[:, :], T.x[:, :]).then_inc(S.xl, 16)
+
+    g.iota(T.ia[:, :], [[0, 32]], 0, 1).then_inc(S.iot, 1)
+    g.iota(T.ic[:, :], [[16, 32]], 0, 0).then_inc(S.iot, 1)
+    V.wait_ge(S.iot, 2)
+    V.tensor_scalar(T.ib[:, :], T.ia[:, :], 15, None, AluOpType.bitwise_and).then_inc(S.ibs, 1)
+    V.wait_ge(S.ibs, 1)
+    V.tensor_tensor(T.lin[:, :], T.ib[:, :], T.ic[:, :], add).then_inc(S.lns, 1)
+    V.wait_ge(S.srow, 16)
+    V.tensor_scalar(T.self5[:, :], T.selo[:, :], 512.0, None, mul).then_inc(S.scs, 1)
+    g.wait_ge(S.scs, 1)
+    g.partition_broadcast(T.selb[:, :], T.self5[:, :], 128).then_inc(S.sbs, 1)
+    g.wait_ge(S.sbs, 1)
+    wants = oth[:4]
+    per = len(eng) // len(wants)
+    trs = []
+    for i, q in enumerate(wants):
+        ad = topo.addr(cores[q])
+        c = _others(groups, q).index(r) - 2
+        trs.append(RemoteDMATransfer(dst_ids=[DstId(rid=ad[0], pnc=ad[1])], remote_sem=S.sela,
+                                     dma_engine_mask=sum(1 << e for e in eng[per * i:per * i + per]),
+                                     srcs=[T.selb[:, q:q + 1]], dsts=[T.sland[:, c:c + 1]]))
+    g.remote_dma_fused(trs, local_sem=S.sent)
+    sent[0] += per * len(wants)
+
+    V.wait_ge(S.lst, 128)
+    V.tensor_scalar(T.soff[:, :], T.sendl[:, :], 4.0, 0.0, mul, AluOpType.max).then_inc(S.sos, 1)
+
+    first = prev[0]
+    rot = 2 * CAPP * _base(groups, r)
+    both = prev + groups[ci]
+
+    def block(q, e=0):
+        return (q - first) % N + N * e
+
+    V.wait_ge(S.pl, 32)
+    terms, nf = [T.plc], [0]
+
+    def term(src, *a):
+        o = T["f%d" % nf[0]]
+        nf[0] += 1
+        V.tensor_scalar(o[:, :], src[:, :], *a).then_inc(S.fs0, 1)
+        terms.append(o)
+
+    term(T.ofl, float(NS), float(-rot - NS * first), mul, add)
+    if rot:
+        term(T.plc, float(rot), float(NS), AluOpType.is_lt, mul)
+    if first:
+        term(T.ofl, float(first), float(N * NS), AluOpType.is_lt, mul)
+    V.wait_ge(S.sbs, 1)
+    V.tensor_scalar(T.selk[:, :], T.selb[0:16, 0:8], float(N * NS // 512), None, mul).then_inc(S.sks, 1)
+    V.wait_ge(S.sks, 1)
+    for q in both:
+        term(T.ofl, float(q), T.selk[:, q:q + 1], AluOpType.is_equal, mul)
+    V.wait_ge(S.fs0, len(terms) - 1)
+    lvl = 1
+    while len(terms) > 1:
+        new = []
+        for i in range(0, len(terms) - 1, 2):
+            o = T["f%d" % nf[0]]
+            nf[0] += 1
+            V.tensor_tensor(o[:, :], terms[i][:, :], terms[i + 1][:, :], add).then_inc(S["fs%d" % lvl], 1)
+            new.append(o)
+        V.wait_ge(S["fs%d" % lvl], len(new))
+        terms = new + terms[2 * len(new):]
+        lvl += 1
+    V.tensor_copy(T.pu[:, :], terms[0][:, :]).then_inc(S.fs4, 1)
+    Y.wait_ge(S.fs4, 1)
+    for k in range(8):
+        Y.dma_start(T.poff[16 * k:16 * k + 16, :], T.pu[:, :]).then_inc(S.pr, 16)
+
+    V.wait_ge(S.wl, 32)
+    V.quantize_mx(T.w_c[:, :], T.w_s[:, :], T.ws[:, :]).then_inc(S.wq, 1)
+    g.wait_ge(S.wq, 1)
+    chip_write(rel, T.xr_c[:, :].bitcast(U8), T.w_c[:, :].bitcast(U8), S.rec)
+    chip_write(rel, T.xr_s[:, :], T.w_s[:, :], S.res)
+
+    V.wait_ge(S.sos, 1)
+    A.wait_ge(S.sos, 1)
+    V.wait_ge(S.xl, 16)
+    A.wait_ge(S.xl, 16)
+
+    def tokens(k, nv):
+        tile = T["tk%d" % k]
+        if k:
+            q = groups[(ci + k) % C][0]
+            runs = [(0, 768, 6 * q, 6 * q + 12)]
+        else:
+            runs = [(384 * b, 384 * b + 384, 6 * q, 6 * q + 6) for b, q in enumerate([r, mate] if mine else [mate, r])]
+        for t in range(4):
+            for c0, c1, l0, l1 in runs:
+                win = T.xs[:, t:4 * TK].indirect(T.soff[:, l0:l1])
+                if t < nv:
+                    V.tensor_copy(tile[:, c0 + t:c1:4], win).then_inc(S["vg%d" % k], 1)
+                else:
+                    A.activation(tile[:, c0 + t:c1:4], win, Copy).then_inc(S["sg%d" % k], 1)
+        if nv:
+            V.wait_ge(S["vg%d" % k], nv * len(runs))
+        V.wait_ge(S["sg%d" % k], (4 - nv) * len(runs))
+        qc, qs, c = (T["q%d_c" % k], T["q%d_s" % k], 0) if k else (T.r_c, T.r_s, 3 * CAPP * mine)
+        V.quantize_mx(qc[:, c:c + 192], qs[:, c:c + 192], tile[:, :]).then_inc(S["tq%d" % k], 1)
+        g.wait_ge(S["tq%d" % k], 1)
+        if k == 0:
+            c, h = 4 * CAPP * mine, _slot_col(groups, mate, r)
+            chip_write(cores[mate], T.r_c[:, h:h + 96].bitcast(U8), T.r_c[:, c:c + 96].bitcast(U8), S.tokM)
+            chip_write(cores[mate], T.r_s[:, h:h + 96], T.r_s[:, c:c + 96], S.tokM)
+            return
+        to = [(d, _slot_col(groups, d, r), 96 * b) for b, d in enumerate(groups[(ci + k) % C])]
+        sem = S["tok%d" % k]
+        _pair(g, T, topo, sent, eng, [(d, T.r_c[:, h:h + 96].bitcast(U8), qc[:, b:b + 96].bitcast(U8), sem) for d, h, b in to])
+        _pair(g, T, topo, sent, eng, [(d, T.r_s[:, h:h + 96], qs[:, b:b + 96], sem) for d, h, b in to])
+
+    tokens(TORD[0], 2)
+    chip_write(cores[mate], T.m_c[:, :].bitcast(U8), T.w_c[:, :].bitcast(U8), S.me)
+    chip_write(cores[mate], T.m_s[:, :], T.w_s[:, :], S.me)
+    tokens(TORD[1], 2)
+    tokens(TORD[2], 2)
+
+    V.wait_ge(S.sela, per * len(wants))
+    V.wait_ge(S.lns, 1)
+    for k in EORD:
+        for b in range(2):
+            j = 2 * (k - 2) + b
+            V.tensor_scalar(T["eo%d" % k][:, 32 * b:32 * b + 32], T.lin[:, :], T.sland[:, j:j + 1], 0.0,
+                            add, AluOpType.max).then_inc(S["eos%d" % k], 1)
+    tokens(0, 0)
+    A.wait_ge(S.wl, 32)
+    for k in EORD:
+        eo, et = T["eo%d" % k], T["et%d" % k]
+        xc, xp = T["x%d_c" % k], T["x%d_s" % k]
+        V.wait_ge(S["eos%d" % k], 2)
+        A.wait_ge(S["eos%d" % k], 2)
+        A.activation(et[:, 0:16 * SP], T.ws[:, :].indirect(eo[:, 0:SP]), Copy).then_inc(S["sge%d" % k], 1)
+        V.tensor_copy(et[:, 16 * SP:1024], T.ws[:, :].indirect(eo[:, SP:64])).then_inc(S["vge%d" % k], 1)
+        V.wait_ge(S["vge%d" % k], 1)
+        V.wait_ge(S["sge%d" % k], 1)
+        V.quantize_mx(xc[:, :], xp[:, :], et[:, :]).then_inc(S["eq%d" % k], 1)
+        g.wait_ge(S["eq%d" % k], 1)
+        chip_write(rel, xc[:, 128:256].bitcast(U8), xc[:, 128:256].bitcast(U8), S["rec%d" % k])
+        chip_write(rel, xp[:, 128:256], xp[:, 128:256], S["res%d" % k])
+        _chosen(g, r, k, 0, False, groups, T, topo, sent, eng)
+        _chosen(g, r, k, 0, True, groups, T, topo, sent, eng)
+
+    g.wait_ge(S.un, 2 * len(eng))
+    chip_write(cores[mate], T.u_c[:, 256:512].bitcast(U8), T.u_c[:, 0:256].bitcast(U8), S.us)
+    chip_write(cores[mate], T.u_s[:, 256:512], T.u_s[:, 0:256], S.us)
+
+    blocks = [(block(r), T.w_c, T.w_s, 0, S.wq, 1), (block(r, 1), T.w_c, T.w_s, 128, None, 0),
+              (block(mate), T.m_c, T.m_s, 0, S.me, 2 * len(ups)), (block(mate, 1), T.m_c, T.m_s, 128, None, 0)]
+
+    def chosen(k):
+        for q in groups[(ci - k) % C]:
+            j = oth.index(q)
+            blocks.append((block(q), T.e_c, T.e_s, 128 * j, S["ex%d" % j], 2 * len(eng)))
+
+    for i, q in enumerate(prev):
+        blocks.append((block(q, mine), T.u_c, T.u_s, 128 * i, S.un, 2 * len(eng)))
+    chosen(EORD[0])
+    for i, q in enumerate(prev):
+        blocks.append((block(q, 1 - mine), T.u_c, T.u_s, 256 + 128 * i, S.us, 2 * len(ups)))
+    chosen(EORD[1])
+
+    half_chips = [[(_base(groups, r) + 2 * hf + j) % C for j in range(2)] for hf in range(2)]
+    h0 = [hf for hf in range(2) if (ci - TORD[-1]) % C not in half_chips[hf]][0]
+    units = ([(i, h0) for i in range(4)] + [(i, 1 - h0) for i in range(4)]
+             + [(i, hf) for i in range(4, len(blocks)) for hf in (h0, 1 - h0)])
+    waited = set()
+
+    def once(sem, cnt):
+        if sem is not None and sem not in waited:
+            waited.add(sem)
+            Te.wait_ge(sem, cnt)
+
+    for u, (i, hf) in enumerate(units):
+        blk, wc, wsc, col, sem, cnt = blocks[i]
+        once(sem, cnt)
+        for c in half_chips[hf]:
+            if c == ci:
+                once(S.tq0, 1)
+                once(S.tokM, 2 * len(ups))
+            else:
+                once(S["tok%d" % ((ci - c) % C)], 2 * len(eng))
+        if u >= 8:
+            Te.wait_ge(S["ev%d" % (u - 8)], 1)
+        b0, c0, p0 = 512 * (u % 8), _half_col(groups, r, hf), NS * blk + HALF * hf
+        Te.matmul_mx(T.ps[:, b0:b0 + HALF], wc[:, col:col + 128], wsc[:, col:col + 128],
+                     T.r_c[:, c0:c0 + HALF], T.r_s[:, c0:c0 + HALF], True, True).then_inc(S["mm%d" % u], 1)
+        ev = S["ev%d" % u] if u < len(units) - 8 else S.evz
+        if u % 2 == 0:
+            V.wait_ge(S["mm%d" % u], 1)
+            V.tensor_copy(T.pw[:, p0:p0 + HALF], T.ps[:, b0:b0 + HALF]).then_inc(ev, 1)
+        else:
+            A.wait_ge(S["mm%d" % u], 1)
+            A.activation(T.pw[:, p0:p0 + HALF], T.ps[:, b0:b0 + HALF], Copy).then_inc(ev, 1)
+
+    for E in (V, A):
+        E.wait_ge(S.pr, 128)
+        E.wait_ge(S.evz, 8)
+    V.tensor_copy(T.yb[:, 0:256], T.pw[:, :].indirect(T.poff[:, 0:16])).then_inc(S.yg, 1)
+    A.activation(T.yb[:, 256:512], T.pw[:, :].indirect(T.poff[:, 16:32]), Copy).then_inc(S.yh, 1)
+    Y.wait_ge(S.yg, 1)
+    Y.dma_start(T.y[:, 0:256], T.yb[:, 0:256]).then_inc(S.y0, 16)
+    A.wait_ge(S.yh, 1)
+    A.dma_start(T.y[:, 256:512], T.yb[:, 256:512]).then_inc(S.y1, 16)
+    Y.wait_ge(S.y0, 16)
+    A.wait_ge(S.y1, 16)
+    g.wait_ge(S.sent, sent[0])

@@ -3,10 +3,25 @@ from concourse.mybir import dt, AluOpType, ActivationFunctionType
 
 N, CAPP, TK = 8, 96, 512
 NS = N * CAPP
-HALF = NS // 2
-SP = 40
-TORD = (1, 3, 2)
-EORD = (3, 2)
+PAIR = 2 * CAPP
+PLAN = dict(
+    both=True,
+    lay=[0, 2, 1, 3],
+    tiles={"t1": ["10", "11"], "t3": ["30", "31"], "t2": ["20", "21"],
+           "ea": ["11", "31"], "eb": ["21", "10"], "ec": ["30", "20"], "ed": ["01", "00"]},
+    way={"t1": "BB", "t3": "DM", "t2": "DD", "ea": "BM", "eb": "BD", "ec": "DD"},
+    apart=["ec"],
+    sel={"D": [[1, 3], [2]], "B": []},
+    vec="T t1.0 t1.1 t1 t3.0 t2.0 t3 t2.1 t0.0 t2 w oa ob t0 oc ea.v ea eb.v eb ec.v ec S",
+    ahead=300,
+    act="t1.2 t1.3 t3.1 t3.2 t3.3 t2.2 t2.3 t0.1 t0.2 t0.3 ea.a eb.a ec.a",
+    send="t1 t3 t2 w t0 ea eb ec",
+    share={"ea": 50, "eb": 44, "ec": 42, "ed": 40},
+    cut={"0": (0, 384), "1": (384, 768), "2": (384, 576), "3": (576, 768), "4": (0, 192), "5": (192, 384)},
+    units="w0.0 w1.0 m0.0 m1.0 w0.1 w1.1 m0.1 m1.1 10.0 10.1 11.0 11.1 31.0 31.1 30.0 30.1 21.0 21.1 20.0 20.2 20.3",
+    stores=2,
+)
+NT = 10
 SCRATCH = {
     "xs": ("sbuf", [128, 4 * TK], "bfloat16"),
     "ws": ("sbuf", [128, 1024], "bfloat16"),
@@ -18,12 +33,8 @@ SCRATCH = {
     "w_s": ("sbuf", [128, 256], "uint8"),
     "m_c": ("sbuf", [128, 256], "float8_e4m3fn_x4"),
     "m_s": ("sbuf", [128, 256], "uint8"),
-    "u_c": ("sbuf", [128, 512], "float8_e4m3fn_x4"),
-    "u_s": ("sbuf", [128, 512], "uint8"),
-    "e_c": ("sbuf", [128, 512], "float8_e4m3fn_x4"),
-    "e_s": ("sbuf", [128, 512], "uint8"),
-    "xr_c": ("sbuf", [128, 256], "float8_e4m3fn_x4"),
-    "xr_s": ("sbuf", [128, 256], "uint8"),
+    "a_c": ("sbuf", [128, 128 * N], "float8_e4m3fn_x4"),
+    "a_s": ("sbuf", [128, 128 * N], "uint8"),
     "ia": ("sbuf", [128, 32], "int32"),
     "ib": ("sbuf", [128, 32], "int32"),
     "ic": ("sbuf", [128, 32], "int32"),
@@ -31,36 +42,34 @@ SCRATCH = {
     "selo": ("sbuf", [1, 16], "int32"),
     "self5": ("sbuf", [1, 16], "float32"),
     "selb": ("sbuf", [128, 16], "float32"),
-    "sland": ("sbuf", [128, 4], "float32"),
+    "sland": ("sbuf", [128, 8], "float32"),
     "selk": ("sbuf", [16, 8], "float32"),
     "plc": ("sbuf", [16, 32], "int32"),
     "ofl": ("sbuf", [16, 32], "int32"),
+    "terms": ("sbuf", [16, 32 * NT], "float32"),
+    "keep": ("sbuf", [16, 32 * NT], "float32"),
+    "sums": ("sbuf", [16, 32 * NT], "float32"),
     "pu": ("sbuf", [16, 32], "uint16"),
     "poff": ("sbuf", [128, 32], "uint16"),
     "ps": ("psum", [128, 4096], "float32"),
-    "pw": ("sbuf", [128, 12 * NS], "float32"),
+    "pw": ("sbuf", [128, (N + 2) * NS], "float32"),
     "yb": ("sbuf", [128, TK], "float32"),
 }
-for _k in range(14):
-    SCRATCH["f%d" % _k] = ("sbuf", [16, 32], "float32")
-for _k in range(4):
-    SCRATCH["tk%d" % _k] = ("sbuf", [128, 768], "bfloat16")
-for _k in range(1, 4):
-    SCRATCH["q%d_c" % _k] = ("sbuf", [128, 192], "float8_e4m3fn_x4")
-    SCRATCH["q%d_s" % _k] = ("sbuf", [128, 192], "uint8")
-for _k in (2, 3):
-    SCRATCH["et%d" % _k] = ("sbuf", [128, 1024], "bfloat16")
-    SCRATCH["eo%d" % _k] = ("sbuf", [128, 64], "uint16")
-    SCRATCH["x%d_c" % _k] = ("sbuf", [128, 256], "float8_e4m3fn_x4")
-    SCRATCH["x%d_s" % _k] = ("sbuf", [128, 256], "uint8")
+TILES = ["t0", "t1", "t2", "t3", "ea", "eb", "ec", "ed"]
+for _t in TILES:
+    _n = PAIR if _t[0] == "t" else 256
+    SCRATCH[_t + "_g"] = ("sbuf", [128, 4 * _n], "bfloat16")
+    SCRATCH[_t + "_c"] = ("sbuf", [128, _n], "float8_e4m3fn_x4")
+    SCRATCH[_t + "_s"] = ("sbuf", [128, _n], "uint8")
+    if _t[0] == "e":
+        SCRATCH[_t + "_o"] = ("sbuf", [128, 64], "uint16")
 
-SEMAPHORES = (["srow", "lst", "xl", "wl", "pl", "iot", "ibs", "lns", "scs", "sbs", "sos", "wq", "sela", "sks", "sent",
-               "me", "un", "us", "tokM", "pr", "yg", "yh", "y0", "y1", "rec", "res", "evz"]
-              + ["fs%d" % k for k in range(5)] + ["tok%d" % k for k in range(1, 4)]
-              + ["%s%d" % (s, k) for k in range(4) for s in ("tq", "vg", "sg")]
-              + ["%s%d" % (s, k) for k in (2, 3) for s in ("eos", "vge", "sge", "eq", "rec", "res")]
-              + ["ex%d" % j for j in range(4)]
-              + ["mm%d" % i for i in range(24)] + ["ev%d" % i for i in range(16)])
+SEMAPHORES = (["srow", "lst", "xl", "wl", "pl", "iot", "ibs", "lns", "scs", "sbs", "sos", "w_q", "sel1", "sel2", "sel3", "selr", "selm",
+               "sks", "sent", "kp0", "kp1", "trm", "scn", "pus", "pr", "me", "evz", "ys"]
+              + ["tok%d" % k for k in range(4)] + ["ex%d" % q for q in range(N)] + ["yg%d" % i for i in range(4)]
+              + ["%s_%s" % (t, s) for t in TILES for s in ("v", "a", "q", "c", "s")] + ["e%s_o" % x for x in "abcd"]
+              + ["%s_%s" % (t, s) for t in TILES if t not in ("t0", "ed") for s in ("c1", "s1")]
+              + ["mm%d" % i for i in range(28)] + ["ev%d" % i for i in range(20)])
 
 
 def _groups(cores, topo):
@@ -76,82 +85,132 @@ def _groups(cores, topo):
 
 
 def _where(groups, q):
-    return [i for i in range(len(groups)) if q in groups[i]][0]
+    c = [i for i in range(len(groups)) if q in groups[i]][0]
+    return c, groups[c].index(q)
+
+
+def _peer(groups, q, part, sign):
+    c, mine = _where(groups, q)
+    return groups[(c + sign * int(part[0])) % len(groups)][int(part[1]) ^ mine]
 
 
 def _relay(cores, groups, q, topo):
     able = [c for c in topo.cores_of(cores[q]) if topo.die(c) != topo.die(cores[q]) and c not in cores
             and all(topo.may_write(c, d) for d in cores)]
-    return able[groups[_where(groups, q)].index(q)]
+    return able[_where(groups, q)[1]]
 
 
-def _others(groups, q):
-    c, n = _where(groups, q), len(groups)
-    return [s for d in range(1, n) for s in groups[(c + d) % n]]
+def _door(cores, groups, q, topo):
+    able = [c for c in range(topo.CHIPS * topo.CORES_PER_CHIP) if topo.mates(topo.chip(c), topo.chip(cores[q]))
+            and topo.die(c) == topo.die(cores[q]) and topo.may_write(c, cores[q])]
+    return able[_where(groups, q)[1]]
 
 
-def _base(groups, q):
-    c = _where(groups, q)
-    return (c - groups[c].index(q)) % len(groups)
-
-
-def _half_col(groups, q, hf):
-    second = groups[_where(groups, q)].index(q)
-    return hf * (HALF + CAPP) if second else CAPP + hf * HALF
+def _pos(groups, q, s):
+    (cq, second), (cs, b) = _where(groups, q), _where(groups, s)
+    i = PLAN["lay"].index((cq - cs) % len(groups))
+    return PAIR * (i if second else len(groups) - 1 - i) + CAPP * (b if i else 1 - b)
 
 
 def _slot_col(groups, q, s):
-    c = _where(groups, s)
-    p = CAPP * (2 * ((c - _base(groups, q)) % len(groups)) + groups[c].index(s))
-    return _half_col(groups, q, p // HALF) + p % HALF
+    return CAPP * _where(groups, q)[1] + _pos(groups, q, s)
 
 
-def _write(g, T, topo, sent, es, to, d, s, sem):
-    ad = topo.addr(to)
-    g.remote_dma(d, s, sem, T.sem.sent, ad[1], ad[0], sum(1 << e for e in es))
-    sent[0] += len(es)
+def _share(tile, i, eng):
+    way = PLAN["way"][tile]
+    return len(eng) // (1 if tile in PLAN["apart"] else len([w for w in way if (w == "B") == (way[i] == "B")]))
 
 
-def _pair(g, T, topo, sent, eng, trs):
-    half = len(eng) // 2
-    out = []
-    for i, (q, d, s, sem) in enumerate(trs):
-        ad = topo.addr(T.cores[q])
-        out.append(RemoteDMATransfer(dst_ids=[DstId(rid=ad[0], pnc=ad[1])], remote_sem=sem, srcs=[s], dsts=[d],
-                                     dma_engine_mask=sum(1 << e for e in eng[half * i:half * i + half])))
-    g.remote_dma_fused(out, local_sem=T.sem.sent)
-    sent[0] += 2 * half
+def _landed(tile, i, eng):
+    return 2 * (len(eng) if PLAN["way"][tile][i] == "M" else _share(tile, i, eng))
 
 
-def _chosen(g, r, k, b, plane, groups, T, topo, sent, eng):
-    d = groups[(_where(groups, r) + k) % len(groups)][b]
-    j = _others(groups, d).index(r)
-    sem = T.sem["ex%d" % j]
-    if plane:
-        _write(g, T, topo, sent, eng, T.cores[d], T.e_s[:, 128 * j:128 * j + 128],
-               T["x%d_s" % k][:, 128 * b:128 * b + 128], sem)
+def _source(groups, r, tile, i):
+    if tile[0] == "t":
+        return CAPP, CAPP * _where(groups, _peer(groups, r, PLAN["tiles"][tile][i], 1))[1]
+    return 128, 128 * i
+
+
+def _landing(groups, r, d, tile):
+    if tile[0] == "t":
+        return "r_", _slot_col(groups, d, r), "tok" + tile[1]
+    return "a_", 128 * r, "ex%d" % r
+
+
+def _bytes(side, *views):
+    return [v.bitcast(dt.uint8) if side == "c" else v for v in views]
+
+
+def _call(g, T, topo, sent, eng, trs):
+    per = len(eng) // len(trs)
+    if len(trs) == 1:
+        c, d, s, sem = trs[0]
+        ad = topo.addr(c)
+        g.remote_dma(d, s, sem, T.sem.sent, ad[1], ad[0], sum(1 << e for e in eng))
     else:
-        _write(g, T, topo, sent, eng, T.cores[d], T.e_c[:, 128 * j:128 * j + 128].bitcast(dt.uint8),
-               T["x%d_c" % k][:, 128 * b:128 * b + 128].bitcast(dt.uint8), sem)
+        out = []
+        for i, (c, d, s, sem) in enumerate(trs):
+            ad = topo.addr(c)
+            out.append(RemoteDMATransfer(dst_ids=[DstId(rid=ad[0], pnc=ad[1])], remote_sem=sem, srcs=[s], dsts=[d],
+                                         dma_engine_mask=sum(1 << e for e in eng[per * i:per * i + per])))
+        g.remote_dma_fused(out, local_sem=T.sem.sent)
+    sent[0] += per * len(trs)
+
+
+def _out(g, T, topo, groups, sent, eng, r, tile, ways, wait=0):
+    for side, only in [(s, i) for i in ((0, 1) if tile in PLAN["apart"] else (None,)) for s in "cs"]:
+        trs = []
+        for i, part in enumerate(PLAN["tiles"][tile]):
+            w = PLAN["way"][tile][i]
+            if w in ways and only in (None, i):
+                d = _peer(groups, r, part, 1)
+                (n, c), (to, h, sem) = _source(groups, r, tile, i), _landing(groups, r, d, tile)
+                dst, src = _bytes(side, T[to + side][:, h:h + n], T[tile + "_" + side][:, c:c + n])
+                if w == "M":
+                    trs.append((_door(T.cores, groups, d, topo), dst, src, T.sem[tile + "_" + side + "1" * i]))
+                else:
+                    trs.append((T.cores[d], dst, src, T.sem[sem]))
+        if trs:
+            if wait:
+                g.wait_ge(T.sem[tile + "_" + side], wait)
+            _call(g, T, topo, sent, eng, trs)
+
+
+def _sel(g, T, topo, groups, sent, eng, r, way):
+    for ks in PLAN["sel"][way]:
+        qs = [q for k in ks for q in groups[(_where(groups, r)[0] - k) % len(groups)]]
+        _call(g, T, topo, sent, eng, [(T.cores[q], T.sland[:, r:r + 1], T.selb[:, q:q + 1], T.sem["sel%d" % ks[0]]) for q in qs])
+
+
+def _engines(core, r, groups, T, topo):
+    eng = topo.engines(core, T.cores[_peer(groups, r, "10", 1)])
+    return eng, [e for e in topo.engines(core, T.cores[_peer(groups, r, "01", 1)]) if e not in eng]
 
 
 def _relay_program(g, core, r, groups, T, topo):
     sent = [0]
-    eng = topo.engines(core, T.cores[_others(groups, r)[0]])
-    ups = [e for e in topo.engines(core, T.cores[r]) if e not in eng]
-    ci = _where(groups, r)
-    j = 128 * groups[ci].index(r)
-    to = groups[(ci + 1) % len(groups)]
-    g.wait_ge(T.sem.rec, len(ups))
-    _pair(g, T, topo, sent, eng, [(d, T.u_c[:, j:j + 128].bitcast(dt.uint8), T.xr_c[:, 128 * b:128 * b + 128].bitcast(dt.uint8),
-                                   T.sem.un) for b, d in enumerate(to)])
-    g.wait_ge(T.sem.res, len(ups))
-    _pair(g, T, topo, sent, eng, [(d, T.u_s[:, j:j + 128], T.xr_s[:, 128 * b:128 * b + 128], T.sem.un) for b, d in enumerate(to)])
-    for k in EORD:
-        g.wait_ge(T.sem["rec%d" % k], len(ups))
-        _chosen(g, r, k, 1, False, groups, T, topo, sent, eng)
-        g.wait_ge(T.sem["res%d" % k], len(ups))
-        _chosen(g, r, k, 1, True, groups, T, topo, sent, eng)
+    eng, ups = _engines(core, r, groups, T, topo)
+    if PLAN["sel"]["B"]:
+        g.wait_ge(T.sem.selr, len(ups))
+        _sel(g, T, topo, groups, sent, eng, r, "B")
+    for tile in PLAN["send"].split():
+        if tile in PLAN["way"]:
+            _out(g, T, topo, groups, sent, eng, r, tile, "B", len(ups))
+    g.wait_ge(T.sem.sent, sent[0])
+
+
+def _door_program(g, core, d, groups, T, topo):
+    sent = [0]
+    eng = topo.engines(core, T.cores[d])
+    for tile in PLAN["send"].split():
+        for side in "cs":
+            for i, w in enumerate(PLAN["way"].get(tile, "")):
+                if w == "M":
+                    s = _peer(groups, d, PLAN["tiles"][tile][i], -1)
+                    n, (to, h, sem) = _source(groups, s, tile, i)[0], _landing(groups, s, d, tile)
+                    g.wait_ge(T.sem[tile + "_" + side + "1" * i], _share(tile, i, eng))
+                    view, = _bytes(side, T[to + side][:, h:h + n])
+                    _call(g, T, topo, sent, eng, [(T.cores[d], view, view, T.sem[sem])])
     g.wait_ge(T.sem.sent, sent[0])
 
 
@@ -164,238 +223,216 @@ def rank_program(g, core, T, topo):
         for q in range(N):
             if _relay(cores, groups, q, topo) == core:
                 _relay_program(g, core, q, groups, T, topo)
+            if _door(cores, groups, q, topo) == core:
+                _door_program(g, core, q, groups, T, topo)
         return
 
-    ci = _where(groups, r)
-    mine = groups[ci].index(r)
-    mate = [q for q in groups[ci] if q != r][0]
-    oth = _others(groups, r)
-    prev = groups[(ci - 1) % C]
+    both = PLAN["both"]
+    ci, mine = _where(groups, r)
+    mate = groups[ci][1 - mine]
     rel = _relay(cores, groups, r, topo)
     S = T.sem
     V, A, Te, Y = g.vector, g.scalar, g.tensor, g.sync
+    queue = {"g": g, "V": V, "A": A, "T": Te}
     Copy = ActivationFunctionType.Copy
-    U8 = dt.uint8
     add, mul = AluOpType.add, AluOpType.mult
-    eng = topo.engines(core, cores[oth[0]])
-    ups = [e for e in topo.engines(core, cores[mate]) if e not in eng]
+    eng, ups = _engines(core, r, groups, T, topo)
     sent = [0]
+    seen = set()
 
-    def chip_write(to, d, s, sem):
-        _write(g, T, topo, sent, ups, to, d, s, sem)
+    def once(q, sem, cnt):
+        if (q, sem) not in seen:
+            seen.add((q, sem))
+            queue[q].wait_ge(S[sem], cnt)
+
+    def chip_write(to, dst, h, src, c, n, sems):
+        for side, sem in zip("cs", sems):
+            _call(g, T, topo, sent, ups, [(to, *_bytes(side, T[dst + side][:, h:h + n], T[src + side][:, c:c + n]), S[sem])])
 
     Y.dma_start(T.selo[0:1, 0:16], T.sel[:, :]).then_inc(S.srow, 16)
-    A.dma_start(T.plc[:, :], T.place[:, :]).then_inc(S.pl, 16)
-    A.dma_start(T.ofl[:, :], T["of"][:, :]).then_inc(S.pl, 16)
     for k in range(4):
         Y.dma_start(T.sendl[16 * k:16 * k + 16, :], T.send[:, :]).then_inc(S.lst, 16)
         A.dma_start(T.sendl[64 + 16 * k:80 + 16 * k, :], T.send[:, :]).then_inc(S.lst, 16)
+    A.dma_start(T.plc[:, :], T.place[:, :]).then_inc(S.pl, 16)
+    Y.dma_start(T.ofl[:, :], T["of"][:, :]).then_inc(S.pl, 16)
+    Y.dma_start(T.xs[:, :], T.x[:, :]).then_inc(S.xl, 16)
     for e in range(2):
         Y.dma_start(T.ws[:, 512 * e:512 * e + 512], T.w[128 * e:128 * e + 128, :]).then_inc(S.wl, 16)
-    A.dma_start(T.xs[:, :], T.x[:, :]).then_inc(S.xl, 16)
 
     g.iota(T.ia[:, :], [[0, 32]], 0, 1).then_inc(S.iot, 1)
     g.iota(T.ic[:, :], [[16, 32]], 0, 0).then_inc(S.iot, 1)
+    shift = [_pos(groups, r, s) - CAPP * s for s in range(N)]
+    steps = [s for s in range(1, N) if shift[s] != shift[s - 1]]
+    nt = 2 + len(steps) + 2 * both
+    V.memset(T.keep[:, 0:32 * nt], 1.0).then_inc(S.kp0, 1)
     V.wait_ge(S.iot, 2)
     V.tensor_scalar(T.ib[:, :], T.ia[:, :], 15, None, AluOpType.bitwise_and).then_inc(S.ibs, 1)
+    V.wait_ge(S.kp0, 1)
+    V.memset(T.keep[:, 0:32 * nt:nt], 0.0).then_inc(S.kp1, 1)
     V.wait_ge(S.ibs, 1)
     V.tensor_tensor(T.lin[:, :], T.ib[:, :], T.ic[:, :], add).then_inc(S.lns, 1)
     V.wait_ge(S.srow, 16)
-    V.tensor_scalar(T.self5[:, :], T.selo[:, :], 512.0, None, mul).then_inc(S.scs, 1)
+    V.tensor_scalar(T.self5[:, :], T.selo[:, :], 512.0, 0.0, mul, AluOpType.max).then_inc(S.scs, 1)
     g.wait_ge(S.scs, 1)
     g.partition_broadcast(T.selb[:, :], T.self5[:, :], 128).then_inc(S.sbs, 1)
     g.wait_ge(S.sbs, 1)
-    wants = oth[:4]
-    per = len(eng) // len(wants)
-    trs = []
-    for i, q in enumerate(wants):
-        ad = topo.addr(cores[q])
-        c = _others(groups, q).index(r) - 2
-        trs.append(RemoteDMATransfer(dst_ids=[DstId(rid=ad[0], pnc=ad[1])], remote_sem=S.sela,
-                                     dma_engine_mask=sum(1 << e for e in eng[per * i:per * i + per]),
-                                     srcs=[T.selb[:, q:q + 1]], dsts=[T.sland[:, c:c + 1]]))
-    g.remote_dma_fused(trs, local_sem=S.sent)
-    sent[0] += per * len(wants)
+    if PLAN["sel"]["B"]:
+        _call(g, T, topo, sent, ups, [(rel, T.selb[:, 0:N], T.selb[:, 0:N], S.selr)])
+    _sel(g, T, topo, groups, sent, eng, r, "D")
+    if not both:
+        _call(g, T, topo, sent, ups, [(cores[mate], T.sland[:, r:r + 1], T.selb[:, mate:mate + 1], S.selm)])
 
     V.wait_ge(S.lst, 128)
     V.tensor_scalar(T.soff[:, :], T.sendl[:, :], 4.0, 0.0, mul, AluOpType.max).then_inc(S.sos, 1)
 
-    first = prev[0]
-    rot = 2 * CAPP * _base(groups, r)
-    both = prev + groups[ci]
-
     def block(q, e=0):
-        return (q - first) % N + N * e
+        return N + groups[ci].index(q) if e else q
 
-    V.wait_ge(S.pl, 32)
-    terms, nf = [T.plc], [0]
+    def last_offsets():
+        terms = [(T.plc, 1.0, float(shift[0]), mul, add), (T.ofl, float(NS), None, mul)]
+        terms += [(T.plc, float(CAPP * s), float(shift[s] - shift[s - 1]), AluOpType.is_ge, mul) for s in steps]
+        terms += [(T.ofl, float(q), T.selk[:, q:q + 1], AluOpType.is_equal, mul) for q in groups[ci] if both]
+        V.wait_ge(S.pl, 32)
+        for i, (src, *a) in enumerate(terms):
+            if both and i == nt - 2:
+                q = groups[ci][0]
+                once("V", "sbs", 1)
+                V.tensor_scalar(T.selk[:, q:q + 2], T.selb[0:16, q:q + 2], NS * (block(q, 1) - q) / 512.0, None, mul).then_inc(S.sks, 1)
+                V.wait_ge(S.sks, 1)
+            V.tensor_scalar(T.terms[:, i:32 * nt:nt], src[:, :], *a).then_inc(S.trm, 1)
 
-    def term(src, *a):
-        o = T["f%d" % nf[0]]
-        nf[0] += 1
-        V.tensor_scalar(o[:, :], src[:, :], *a).then_inc(S.fs0, 1)
-        terms.append(o)
+    def last_sums():
+        V.wait_ge(S.trm, nt)
+        V.wait_ge(S.kp1, 1)
+        V.tensor_tensor_scan(T.sums[:, 0:32 * nt], T.keep[:, 0:32 * nt], T.terms[:, 0:32 * nt], 0.0, mul, add).then_inc(S.scn, 1)
+        V.wait_ge(S.scn, 1)
+        V.tensor_copy(T.pu[:, :], T.sums[:, nt - 1:32 * nt:nt]).then_inc(S.pus, 1)
+        Y.wait_ge(S.pus, 1)
+        for k in range(8):
+            Y.dma_start(T.poff[16 * k:16 * k + 16, :], T.pu[:, :]).then_inc(S.pr, 16)
 
-    term(T.ofl, float(NS), float(-rot - NS * first), mul, add)
-    if rot:
-        term(T.plc, float(rot), float(NS), AluOpType.is_lt, mul)
-    if first:
-        term(T.ofl, float(first), float(N * NS), AluOpType.is_lt, mul)
-    V.wait_ge(S.sbs, 1)
-    V.tensor_scalar(T.selk[:, :], T.selb[0:16, 0:8], float(N * NS // 512), None, mul).then_inc(S.sks, 1)
-    V.wait_ge(S.sks, 1)
-    for q in both:
-        term(T.ofl, float(q), T.selk[:, q:q + 1], AluOpType.is_equal, mul)
-    V.wait_ge(S.fs0, len(terms) - 1)
-    lvl = 1
-    while len(terms) > 1:
-        new = []
-        for i in range(0, len(terms) - 1, 2):
-            o = T["f%d" % nf[0]]
-            nf[0] += 1
-            V.tensor_tensor(o[:, :], terms[i][:, :], terms[i + 1][:, :], add).then_inc(S["fs%d" % lvl], 1)
-            new.append(o)
-        V.wait_ge(S["fs%d" % lvl], len(new))
-        terms = new + terms[2 * len(new):]
-        lvl += 1
-    V.tensor_copy(T.pu[:, :], terms[0][:, :]).then_inc(S.fs4, 1)
-    Y.wait_ge(S.fs4, 1)
-    for k in range(8):
-        Y.dma_start(T.poff[16 * k:16 * k + 16, :], T.pu[:, :]).then_inc(S.pr, 16)
+    vec, act = PLAN["vec"].split(), PLAN["act"].split()
 
-    V.wait_ge(S.wl, 32)
-    V.quantize_mx(T.w_c[:, :], T.w_s[:, :], T.ws[:, :]).then_inc(S.wq, 1)
-    g.wait_ge(S.wq, 1)
-    chip_write(rel, T.xr_c[:, :].bitcast(U8), T.w_c[:, :].bitcast(U8), S.rec)
-    chip_write(rel, T.xr_s[:, :], T.w_s[:, :], S.res)
-
-    V.wait_ge(S.sos, 1)
-    A.wait_ge(S.sos, 1)
-    V.wait_ge(S.xl, 16)
-    A.wait_ge(S.xl, 16)
-
-    def tokens(k, nv):
-        tile = T["tk%d" % k]
-        if k:
-            q = groups[(ci + k) % C][0]
-            runs = [(0, 768, 6 * q, 6 * q + 12)]
+    def copy(q, out, src, sem):
+        if q == "V":
+            V.tensor_copy(out, src).then_inc(sem, 1)
         else:
-            runs = [(384 * b, 384 * b + 384, 6 * q, 6 * q + 6) for b, q in enumerate([r, mate] if mine else [mate, r])]
-        for t in range(4):
-            for c0, c1, l0, l1 in runs:
-                win = T.xs[:, t:4 * TK].indirect(T.soff[:, l0:l1])
-                if t < nv:
-                    V.tensor_copy(tile[:, c0 + t:c1:4], win).then_inc(S["vg%d" % k], 1)
-                else:
-                    A.activation(tile[:, c0 + t:c1:4], win, Copy).then_inc(S["sg%d" % k], 1)
-        if nv:
-            V.wait_ge(S["vg%d" % k], nv * len(runs))
-        V.wait_ge(S["sg%d" % k], (4 - nv) * len(runs))
-        qc, qs, c = (T["q%d_c" % k], T["q%d_s" % k], 0) if k else (T.r_c, T.r_s, 3 * CAPP * mine)
-        V.quantize_mx(qc[:, c:c + 192], qs[:, c:c + 192], tile[:, :]).then_inc(S["tq%d" % k], 1)
-        g.wait_ge(S["tq%d" % k], 1)
-        if k == 0:
-            c, h = 4 * CAPP * mine, _slot_col(groups, mate, r)
-            chip_write(cores[mate], T.r_c[:, h:h + 96].bitcast(U8), T.r_c[:, c:c + 96].bitcast(U8), S.tokM)
-            chip_write(cores[mate], T.r_s[:, h:h + 96], T.r_s[:, c:c + 96], S.tokM)
-            return
-        to = [(d, _slot_col(groups, d, r), 96 * b) for b, d in enumerate(groups[(ci + k) % C])]
-        sem = S["tok%d" % k]
-        _pair(g, T, topo, sent, eng, [(d, T.r_c[:, h:h + 96].bitcast(U8), qc[:, b:b + 96].bitcast(U8), sem) for d, h, b in to])
-        _pair(g, T, topo, sent, eng, [(d, T.r_s[:, h:h + 96], qs[:, b:b + 96], sem) for d, h, b in to])
+            A.activation(out, src, Copy).then_inc(sem, 1)
 
-    tokens(TORD[0], 2)
-    chip_write(cores[mate], T.m_c[:, :].bitcast(U8), T.w_c[:, :].bitcast(U8), S.me)
-    chip_write(cores[mate], T.m_s[:, :], T.w_s[:, :], S.me)
-    tokens(TORD[1], 2)
-    tokens(TORD[2], 2)
+    def gather(q, name):
+        tile, part = name.split(".")
+        sem = S[tile + "_" + q.lower()]
+        if tile[0] == "t":
+            once(q, "sos", 1)
+            once(q, "xl", 16)
+            t, d = int(part), groups[(ci + int(tile[1])) % C][0]
+            copy(q, T[tile + "_g"][:, t:4 * PAIR:4], T.xs[:, t:4 * TK].indirect(T.soff[:, 6 * d:6 * d + 12]), sem)
+        else:
+            once(q, "wl", 32)
+            once(q, tile + "_o", 2)
+            l0, l1 = (0, PLAN["share"][tile]) if q == "A" else (PLAN["share"][tile], 64)
+            copy(q, T[tile + "_g"][:, 16 * l0:16 * l1], T.ws[:, :].indirect(T[tile + "_o"][:, l0:l1]), sem)
 
-    V.wait_ge(S.sela, per * len(wants))
-    V.wait_ge(S.lns, 1)
-    for k in EORD:
-        for b in range(2):
-            j = 2 * (k - 2) + b
-            V.tensor_scalar(T["eo%d" % k][:, 32 * b:32 * b + 32], T.lin[:, :], T.sland[:, j:j + 1], 0.0,
-                            add, AluOpType.max).then_inc(S["eos%d" % k], 1)
-    tokens(0, 0)
-    A.wait_ge(S.wl, 32)
-    for k in EORD:
-        eo, et = T["eo%d" % k], T["et%d" % k]
-        xc, xp = T["x%d_c" % k], T["x%d_s" % k]
-        V.wait_ge(S["eos%d" % k], 2)
-        A.wait_ge(S["eos%d" % k], 2)
-        A.activation(et[:, 0:16 * SP], T.ws[:, :].indirect(eo[:, 0:SP]), Copy).then_inc(S["sge%d" % k], 1)
-        V.tensor_copy(et[:, 16 * SP:1024], T.ws[:, :].indirect(eo[:, SP:64])).then_inc(S["vge%d" % k], 1)
-        V.wait_ge(S["vge%d" % k], 1)
-        V.wait_ge(S["sge%d" % k], 1)
-        V.quantize_mx(xc[:, :], xp[:, :], et[:, :]).then_inc(S["eq%d" % k], 1)
-        g.wait_ge(S["eq%d" % k], 1)
-        chip_write(rel, xc[:, 128:256].bitcast(U8), xc[:, 128:256].bitcast(U8), S["rec%d" % k])
-        chip_write(rel, xp[:, 128:256], xp[:, 128:256], S["res%d" % k])
-        _chosen(g, r, k, 0, False, groups, T, topo, sent, eng)
-        _chosen(g, r, k, 0, True, groups, T, topo, sent, eng)
+    def quantise(tile):
+        for names, s in ((vec, "_v"), (act, "_a")):
+            n = len([a for a in names if a.startswith(tile + ".")])
+            if n:
+                V.wait_ge(S[tile + s], n)
+        if tile == "t0":
+            c = (NS - CAPP) * (1 - mine)
+            V.quantize_mx(T.r_c[:, c:c + PAIR], T.r_s[:, c:c + PAIR], T.t0_g[:, :]).then_inc(S.t0_q, 1)
+        else:
+            V.quantize_mx(T[tile + "_c"][:, :], T[tile + "_s"][:, :], T[tile + "_g"][:, :]).then_inc(S[tile + "_q"], 1)
 
-    g.wait_ge(S.un, 2 * len(eng))
-    chip_write(cores[mate], T.u_c[:, 256:512].bitcast(U8), T.u_c[:, 0:256].bitcast(U8), S.us)
-    chip_write(cores[mate], T.u_s[:, 256:512], T.u_s[:, 0:256], S.us)
-
-    blocks = [(block(r), T.w_c, T.w_s, 0, S.wq, 1), (block(r, 1), T.w_c, T.w_s, 128, None, 0),
-              (block(mate), T.m_c, T.m_s, 0, S.me, 2 * len(ups)), (block(mate, 1), T.m_c, T.m_s, 128, None, 0)]
-
-    def chosen(k):
-        for q in groups[(ci - k) % C]:
-            j = oth.index(q)
-            blocks.append((block(q), T.e_c, T.e_s, 128 * j, S["ex%d" % j], 2 * len(eng)))
-
-    for i, q in enumerate(prev):
-        blocks.append((block(q, mine), T.u_c, T.u_s, 128 * i, S.un, 2 * len(eng)))
-    chosen(EORD[0])
-    for i, q in enumerate(prev):
-        blocks.append((block(q, 1 - mine), T.u_c, T.u_s, 256 + 128 * i, S.us, 2 * len(ups)))
-    chosen(EORD[1])
-
-    half_chips = [[(_base(groups, r) + 2 * hf + j) % C for j in range(2)] for hf in range(2)]
-    h0 = [hf for hf in range(2) if (ci - TORD[-1]) % C not in half_chips[hf]][0]
-    units = ([(i, h0) for i in range(4)] + [(i, 1 - h0) for i in range(4)]
-             + [(i, hf) for i in range(4, len(blocks)) for hf in (h0, 1 - h0)])
-    waited = set()
-
-    def once(sem, cnt):
-        if sem is not None and sem not in waited:
-            waited.add(sem)
-            Te.wait_ge(sem, cnt)
-
-    for u, (i, hf) in enumerate(units):
-        blk, wc, wsc, col, sem, cnt = blocks[i]
-        once(sem, cnt)
-        for c in half_chips[hf]:
-            if c == ci:
-                once(S.tq0, 1)
-                once(S.tokM, 2 * len(ups))
+    def offsets(tile):
+        once("V", "lns", 1)
+        for i, part in enumerate(PLAN["tiles"][tile]):
+            d, k = _peer(groups, r, part, 1), int(part[0])
+            if d == r:
+                once("V", "sbs", 1)
+            elif d == mate:
+                once("V", "selm", len(ups))
             else:
-                once(S["tok%d" % ((ci - c) % C)], 2 * len(eng))
+                once("V", "sel%d" % [ks[0] for way in "DB" for ks in PLAN["sel"][way] if k in ks][0], len(eng))
+            V.tensor_scalar(T[tile + "_o"][:, 32 * i:32 * i + 32], T.lin[:, :], (T.selb if d == r else T.sland)[:, d:d + 1], None,
+                            add).then_inc(S[tile + "_o"], 1)
+
+    for name in vec:
+        if name == "T":
+            last_offsets()
+        elif name == "S":
+            last_sums()
+        elif name == "w":
+            once("V", "wl", 32)
+            V.quantize_mx(T.w_c[:, :], T.w_s[:, :], T.ws[:, :]).then_inc(S.w_q, 1)
+        elif name[0] == "o":
+            offsets("e" + name[1])
+        elif "." in name:
+            gather("V", name)
+        else:
+            quantise(name)
+    for name in act:
+        gather("A", name)
+
+    for tile in PLAN["send"].split():
+        g.wait_ge(S[tile + "_q"], 1)
+        if tile == "t0":
+            chip_write(cores[mate], "r_", _slot_col(groups, mate, r), "r_", NS * (1 - mine), CAPP, ["tok0", "tok0"])
+        elif tile == "w":
+            chip_write(cores[mate], "m_", 0, "w_", 0, 256, ["me", "me"])
+        elif tile == "ed":
+            chip_write(cores[mate], "a_", 128 * r, "ed_", 0, 128, ["ex%d" % r] * 2)
+        else:
+            relayed = [_source(groups, r, tile, i) for i, w in enumerate(PLAN["way"][tile]) if w == "B"]
+            if relayed:
+                c = min(c for n, c in relayed)
+                chip_write(rel, tile + "_", c, tile + "_", c, sum(n for n, c in relayed), [tile + "_c", tile + "_s"])
+            _out(g, T, topo, groups, sent, eng, r, tile, "DM")
+
+    def expert(name):
+        if name[0] == "w":
+            return block(r, int(name[1])), "w_", 128 * int(name[1]), "w_q", 1
+        if name[0] == "m":
+            return block(mate, int(name[1])), "m_", 128 * int(name[1]), "me", 2 * len(ups)
+        if name == "00":
+            return r, "ed_", 128, "ed_q", 1
+        q = _peer(groups, r, name, -1)
+        if q == mate:
+            return q, "a_", 128 * q, "ex%d" % q, 2 * len(ups)
+        tile = [t for t in PLAN["way"] if t[0] == "e" and name in PLAN["tiles"][t]][0]
+        return q, "a_", 128 * q, "ex%d" % q, _landed(tile, PLAN["tiles"][tile].index(name), eng)
+
+    units = [u.split(".") for u in PLAN["units"].split()]
+    load = {"V": PLAN["ahead"], "A": 0}
+    for u, (name, piece) in enumerate(units):
+        blk, buf, col, sem, cnt = expert(name)
+        once("T", sem, cnt)
+        c0, c1 = PLAN["cut"][piece]
+        for k in PLAN["lay"][c0 // PAIR:(c1 - 1) // PAIR + 1]:
+            if k == 0:
+                once("T", "t0_q", 1)
+            once("T", "tok%d" % k, sum(_landed("t%d" % k, i, eng) for i in range(2)) if k else 2 * len(ups))
         if u >= 8:
             Te.wait_ge(S["ev%d" % (u - 8)], 1)
-        b0, c0, p0 = 512 * (u % 8), _half_col(groups, r, hf), NS * blk + HALF * hf
-        Te.matmul_mx(T.ps[:, b0:b0 + HALF], wc[:, col:col + 128], wsc[:, col:col + 128],
-                     T.r_c[:, c0:c0 + HALF], T.r_s[:, c0:c0 + HALF], True, True).then_inc(S["mm%d" % u], 1)
-        ev = S["ev%d" % u] if u < len(units) - 8 else S.evz
-        if u % 2 == 0:
-            V.wait_ge(S["mm%d" % u], 1)
-            V.tensor_copy(T.pw[:, p0:p0 + HALF], T.ps[:, b0:b0 + HALF]).then_inc(ev, 1)
-        else:
-            A.wait_ge(S["mm%d" % u], 1)
-            A.activation(T.pw[:, p0:p0 + HALF], T.ps[:, b0:b0 + HALF], Copy).then_inc(ev, 1)
+        p0, n = c0 if mine else NS - c1, c1 - c0
+        b0, c0 = 512 * (u % 8), p0 + CAPP * mine
+        Te.matmul_mx(T.ps[:, b0:b0 + n], T[buf + "c"][:, col:col + 128], T[buf + "s"][:, col:col + 128],
+                     T.r_c[:, c0:c0 + n], T.r_s[:, c0:c0 + n], True, True).then_inc(S["mm%d" % u], 1)
+        q = "V" if load["V"] <= load["A"] else "A"
+        load[q] += n + 64
+        queue[q].wait_ge(S["mm%d" % u], 1)
+        copy(q, T.pw[:, NS * blk + p0:NS * blk + p0 + n], T.ps[:, b0:b0 + n], S["ev%d" % u] if u < len(units) - 8 else S.evz)
 
+    pw = T.pw[:, 0:(N + 2 * both) * NS]
     for E in (V, A):
         E.wait_ge(S.pr, 128)
         E.wait_ge(S.evz, 8)
-    V.tensor_copy(T.yb[:, 0:256], T.pw[:, :].indirect(T.poff[:, 0:16])).then_inc(S.yg, 1)
-    A.activation(T.yb[:, 256:512], T.pw[:, :].indirect(T.poff[:, 16:32]), Copy).then_inc(S.yh, 1)
-    Y.wait_ge(S.yg, 1)
-    Y.dma_start(T.y[:, 0:256], T.yb[:, 0:256]).then_inc(S.y0, 16)
-    A.wait_ge(S.yh, 1)
-    A.dma_start(T.y[:, 256:512], T.yb[:, 256:512]).then_inc(S.y1, 16)
-    Y.wait_ge(S.y0, 16)
-    A.wait_ge(S.y1, 16)
+    n = TK // PLAN["stores"]
+    for i in range(PLAN["stores"]):
+        copy("VA"[i % 2], T.yb[:, n * i:n * i + n], pw.indirect(T.poff[:, n * i // 16:(n * i + n) // 16]), S["yg%d" % i])
+    for i in range(PLAN["stores"]):
+        E = A if i == PLAN["stores"] - 1 else Y
+        E.wait_ge(S["yg%d" % i], 1)
+        E.dma_start(T.y[:, n * i:n * i + n], T.yb[:, n * i:n * i + n]).then_inc(S.ys, 16)
+    Y.wait_ge(S.ys, 16 * PLAN["stores"])
     g.wait_ge(S.sent, sent[0])

from concourse.bass import DstId, RemoteDMATransfer
from concourse.mybir import dt, AluOpType, ActivationFunctionType

N, CAPP, TK = 8, 96, 512
NS = N * CAPP
PAIR = 2 * CAPP
PLAN = dict(
    both=True,
    lay=[0, 2, 1, 3],
    tiles={"t1": ["10", "11"], "t3": ["30", "31"], "t2": ["20", "21"],
           "ea": ["11", "31"], "eb": ["21", "10"], "ec": ["30", "20"], "ed": ["01", "00"]},
    way={"t1": "BB", "t3": "DM", "t2": "DD", "ea": "BM", "eb": "BD", "ec": "DD"},
    apart=["ec"],
    sel={"D": [[1, 3], [2]], "B": []},
    vec="T t1.0 t1.1 t1 t3.0 t2.0 t3 t2.1 t0.0 t2 w oa ob t0 oc ea.v ea eb.v eb ec.v ec S",
    ahead=300,
    act="t1.2 t1.3 t3.1 t3.2 t3.3 t2.2 t2.3 t0.1 t0.2 t0.3 ea.a eb.a ec.a",
    send="t1 t3 t2 w t0 ea eb ec",
    share={"ea": 50, "eb": 44, "ec": 42, "ed": 40},
    cut={"0": (0, 384), "1": (384, 768), "2": (384, 576), "3": (576, 768), "4": (0, 192), "5": (192, 384)},
    units="w0.0 w1.0 m0.0 m1.0 w0.1 w1.1 m0.1 m1.1 10.0 10.1 11.0 11.1 31.0 31.1 30.0 30.1 21.0 21.1 20.0 20.2 20.3",
    stores=2,
)
NT = 10
SCRATCH = {
    "xs": ("sbuf", [128, 4 * TK], "bfloat16"),
    "ws": ("sbuf", [128, 1024], "bfloat16"),
    "sendl": ("sbuf", [128, 48], "int32"),
    "soff": ("sbuf", [128, 48], "uint16"),
    "r_c": ("sbuf", [128, CAPP + NS], "float8_e4m3fn_x4"),
    "r_s": ("sbuf", [128, CAPP + NS], "uint8"),
    "w_c": ("sbuf", [128, 256], "float8_e4m3fn_x4"),
    "w_s": ("sbuf", [128, 256], "uint8"),
    "m_c": ("sbuf", [128, 256], "float8_e4m3fn_x4"),
    "m_s": ("sbuf", [128, 256], "uint8"),
    "a_c": ("sbuf", [128, 128 * N], "float8_e4m3fn_x4"),
    "a_s": ("sbuf", [128, 128 * N], "uint8"),
    "ia": ("sbuf", [128, 32], "int32"),
    "ib": ("sbuf", [128, 32], "int32"),
    "ic": ("sbuf", [128, 32], "int32"),
    "lin": ("sbuf", [128, 32], "float32"),
    "selo": ("sbuf", [1, 16], "int32"),
    "self5": ("sbuf", [1, 16], "float32"),
    "selb": ("sbuf", [128, 16], "float32"),
    "sland": ("sbuf", [128, 8], "float32"),
    "selk": ("sbuf", [16, 8], "float32"),
    "plc": ("sbuf", [16, 32], "int32"),
    "ofl": ("sbuf", [16, 32], "int32"),
    "terms": ("sbuf", [16, 32 * NT], "float32"),
    "keep": ("sbuf", [16, 32 * NT], "float32"),
    "sums": ("sbuf", [16, 32 * NT], "float32"),
    "pu": ("sbuf", [16, 32], "uint16"),
    "poff": ("sbuf", [128, 32], "uint16"),
    "ps": ("psum", [128, 4096], "float32"),
    "pw": ("sbuf", [128, (N + 2) * NS], "float32"),
    "yb": ("sbuf", [128, TK], "float32"),
}
TILES = ["t0", "t1", "t2", "t3", "ea", "eb", "ec", "ed"]
for _t in TILES:
    _n = PAIR if _t[0] == "t" else 256
    SCRATCH[_t + "_g"] = ("sbuf", [128, 4 * _n], "bfloat16")
    SCRATCH[_t + "_c"] = ("sbuf", [128, _n], "float8_e4m3fn_x4")
    SCRATCH[_t + "_s"] = ("sbuf", [128, _n], "uint8")
    if _t[0] == "e":
        SCRATCH[_t + "_o"] = ("sbuf", [128, 64], "uint16")

SEMAPHORES = (["srow", "lst", "xl", "wl", "pl", "iot", "ibs", "lns", "scs", "sbs", "sos", "w_q", "sel1", "sel2", "sel3", "selr", "selm",
               "sks", "sent", "kp0", "kp1", "trm", "scn", "pus", "pr", "me", "evz", "ys"]
              + ["tok%d" % k for k in range(4)] + ["ex%d" % q for q in range(N)] + ["yg%d" % i for i in range(4)]
              + ["%s_%s" % (t, s) for t in TILES for s in ("v", "a", "q", "c", "s")] + ["e%s_o" % x for x in "abcd"]
              + ["%s_%s" % (t, s) for t in TILES if t not in ("t0", "ed") for s in ("c1", "s1")]
              + ["mm%d" % i for i in range(28)] + ["ev%d" % i for i in range(20)])


def _groups(cores, topo):
    out = []
    for q in range(len(cores)):
        for grp in out:
            if topo.chip(cores[grp[0]]) == topo.chip(cores[q]):
                grp.append(q)
                break
        else:
            out.append([q])
    return out


def _where(groups, q):
    c = [i for i in range(len(groups)) if q in groups[i]][0]
    return c, groups[c].index(q)


def _peer(groups, q, part, sign):
    c, mine = _where(groups, q)
    return groups[(c + sign * int(part[0])) % len(groups)][int(part[1]) ^ mine]


def _relay(cores, groups, q, topo):
    able = [c for c in topo.cores_of(cores[q]) if topo.die(c) != topo.die(cores[q]) and c not in cores
            and all(topo.may_write(c, d) for d in cores)]
    return able[_where(groups, q)[1]]


def _door(cores, groups, q, topo):
    able = [c for c in range(topo.CHIPS * topo.CORES_PER_CHIP) if topo.mates(topo.chip(c), topo.chip(cores[q]))
            and topo.die(c) == topo.die(cores[q]) and topo.may_write(c, cores[q])]
    return able[_where(groups, q)[1]]


def _pos(groups, q, s):
    (cq, second), (cs, b) = _where(groups, q), _where(groups, s)
    i = PLAN["lay"].index((cq - cs) % len(groups))
    return PAIR * (i if second else len(groups) - 1 - i) + CAPP * (b if i else 1 - b)


def _slot_col(groups, q, s):
    return CAPP * _where(groups, q)[1] + _pos(groups, q, s)


def _share(tile, i, eng):
    way = PLAN["way"][tile]
    return len(eng) // (1 if tile in PLAN["apart"] else len([w for w in way if (w == "B") == (way[i] == "B")]))


def _landed(tile, i, eng):
    return 2 * (len(eng) if PLAN["way"][tile][i] == "M" else _share(tile, i, eng))


def _source(groups, r, tile, i):
    if tile[0] == "t":
        return CAPP, CAPP * _where(groups, _peer(groups, r, PLAN["tiles"][tile][i], 1))[1]
    return 128, 128 * i


def _landing(groups, r, d, tile):
    if tile[0] == "t":
        return "r_", _slot_col(groups, d, r), "tok" + tile[1]
    return "a_", 128 * r, "ex%d" % r


def _bytes(side, *views):
    return [v.bitcast(dt.uint8) if side == "c" else v for v in views]


def _call(g, T, topo, sent, eng, trs):
    per = len(eng) // len(trs)
    if len(trs) == 1:
        c, d, s, sem = trs[0]
        ad = topo.addr(c)
        g.remote_dma(d, s, sem, T.sem.sent, ad[1], ad[0], sum(1 << e for e in eng))
    else:
        out = []
        for i, (c, d, s, sem) in enumerate(trs):
            ad = topo.addr(c)
            out.append(RemoteDMATransfer(dst_ids=[DstId(rid=ad[0], pnc=ad[1])], remote_sem=sem, srcs=[s], dsts=[d],
                                         dma_engine_mask=sum(1 << e for e in eng[per * i:per * i + per])))
        g.remote_dma_fused(out, local_sem=T.sem.sent)
    sent[0] += per * len(trs)


def _out(g, T, topo, groups, sent, eng, r, tile, ways, wait=0):
    for side, only in [(s, i) for i in ((0, 1) if tile in PLAN["apart"] else (None,)) for s in "cs"]:
        trs = []
        for i, part in enumerate(PLAN["tiles"][tile]):
            w = PLAN["way"][tile][i]
            if w in ways and only in (None, i):
                d = _peer(groups, r, part, 1)
                (n, c), (to, h, sem) = _source(groups, r, tile, i), _landing(groups, r, d, tile)
                dst, src = _bytes(side, T[to + side][:, h:h + n], T[tile + "_" + side][:, c:c + n])
                if w == "M":
                    trs.append((_door(T.cores, groups, d, topo), dst, src, T.sem[tile + "_" + side + "1" * i]))
                else:
                    trs.append((T.cores[d], dst, src, T.sem[sem]))
        if trs:
            if wait:
                g.wait_ge(T.sem[tile + "_" + side], wait)
            _call(g, T, topo, sent, eng, trs)


def _sel(g, T, topo, groups, sent, eng, r, way):
    for ks in PLAN["sel"][way]:
        qs = [q for k in ks for q in groups[(_where(groups, r)[0] - k) % len(groups)]]
        _call(g, T, topo, sent, eng, [(T.cores[q], T.sland[:, r:r + 1], T.selb[:, q:q + 1], T.sem["sel%d" % ks[0]]) for q in qs])


def _engines(core, r, groups, T, topo):
    eng = topo.engines(core, T.cores[_peer(groups, r, "10", 1)])
    return eng, [e for e in topo.engines(core, T.cores[_peer(groups, r, "01", 1)]) if e not in eng]


def _relay_program(g, core, r, groups, T, topo):
    sent = [0]
    eng, ups = _engines(core, r, groups, T, topo)
    if PLAN["sel"]["B"]:
        g.wait_ge(T.sem.selr, len(ups))
        _sel(g, T, topo, groups, sent, eng, r, "B")
    for tile in PLAN["send"].split():
        if tile in PLAN["way"]:
            _out(g, T, topo, groups, sent, eng, r, tile, "B", len(ups))
    g.wait_ge(T.sem.sent, sent[0])


def _door_program(g, core, d, groups, T, topo):
    sent = [0]
    eng = topo.engines(core, T.cores[d])
    for tile in PLAN["send"].split():
        for side in "cs":
            for i, w in enumerate(PLAN["way"].get(tile, "")):
                if w == "M":
                    s = _peer(groups, d, PLAN["tiles"][tile][i], -1)
                    n, (to, h, sem) = _source(groups, s, tile, i)[0], _landing(groups, s, d, tile)
                    g.wait_ge(T.sem[tile + "_" + side + "1" * i], _share(tile, i, eng))
                    view, = _bytes(side, T[to + side][:, h:h + n])
                    _call(g, T, topo, sent, eng, [(T.cores[d], view, view, T.sem[sem])])
    g.wait_ge(T.sem.sent, sent[0])


def rank_program(g, core, T, topo):
    cores = T.cores
    groups = _groups(cores, topo)
    C = len(groups)
    r = T.rank_of(core)
    if r is None:
        for q in range(N):
            if _relay(cores, groups, q, topo) == core:
                _relay_program(g, core, q, groups, T, topo)
            if _door(cores, groups, q, topo) == core:
                _door_program(g, core, q, groups, T, topo)
        return

    both = PLAN["both"]
    ci, mine = _where(groups, r)
    mate = groups[ci][1 - mine]
    rel = _relay(cores, groups, r, topo)
    S = T.sem
    V, A, Te, Y = g.vector, g.scalar, g.tensor, g.sync
    queue = {"g": g, "V": V, "A": A, "T": Te}
    Copy = ActivationFunctionType.Copy
    add, mul = AluOpType.add, AluOpType.mult
    eng, ups = _engines(core, r, groups, T, topo)
    sent = [0]
    seen = set()

    def once(q, sem, cnt):
        if (q, sem) not in seen:
            seen.add((q, sem))
            queue[q].wait_ge(S[sem], cnt)

    def chip_write(to, dst, h, src, c, n, sems):
        for side, sem in zip("cs", sems):
            _call(g, T, topo, sent, ups, [(to, *_bytes(side, T[dst + side][:, h:h + n], T[src + side][:, c:c + n]), S[sem])])

    Y.dma_start(T.selo[0:1, 0:16], T.sel[:, :]).then_inc(S.srow, 16)
    for k in range(4):
        Y.dma_start(T.sendl[16 * k:16 * k + 16, :], T.send[:, :]).then_inc(S.lst, 16)
        A.dma_start(T.sendl[64 + 16 * k:80 + 16 * k, :], T.send[:, :]).then_inc(S.lst, 16)
    A.dma_start(T.plc[:, :], T.place[:, :]).then_inc(S.pl, 16)
    Y.dma_start(T.ofl[:, :], T["of"][:, :]).then_inc(S.pl, 16)
    Y.dma_start(T.xs[:, :], T.x[:, :]).then_inc(S.xl, 16)
    for e in range(2):
        Y.dma_start(T.ws[:, 512 * e:512 * e + 512], T.w[128 * e:128 * e + 128, :]).then_inc(S.wl, 16)

    g.iota(T.ia[:, :], [[0, 32]], 0, 1).then_inc(S.iot, 1)
    g.iota(T.ic[:, :], [[16, 32]], 0, 0).then_inc(S.iot, 1)
    shift = [_pos(groups, r, s) - CAPP * s for s in range(N)]
    steps = [s for s in range(1, N) if shift[s] != shift[s - 1]]
    nt = 2 + len(steps) + 2 * both
    V.memset(T.keep[:, 0:32 * nt], 1.0).then_inc(S.kp0, 1)
    V.wait_ge(S.iot, 2)
    V.tensor_scalar(T.ib[:, :], T.ia[:, :], 15, None, AluOpType.bitwise_and).then_inc(S.ibs, 1)
    V.wait_ge(S.kp0, 1)
    V.memset(T.keep[:, 0:32 * nt:nt], 0.0).then_inc(S.kp1, 1)
    V.wait_ge(S.ibs, 1)
    V.tensor_tensor(T.lin[:, :], T.ib[:, :], T.ic[:, :], add).then_inc(S.lns, 1)
    V.wait_ge(S.srow, 16)
    V.tensor_scalar(T.self5[:, :], T.selo[:, :], 512.0, 0.0, mul, AluOpType.max).then_inc(S.scs, 1)
    g.wait_ge(S.scs, 1)
    g.partition_broadcast(T.selb[:, :], T.self5[:, :], 128).then_inc(S.sbs, 1)
    g.wait_ge(S.sbs, 1)
    if PLAN["sel"]["B"]:
        _call(g, T, topo, sent, ups, [(rel, T.selb[:, 0:N], T.selb[:, 0:N], S.selr)])
    _sel(g, T, topo, groups, sent, eng, r, "D")
    if not both:
        _call(g, T, topo, sent, ups, [(cores[mate], T.sland[:, r:r + 1], T.selb[:, mate:mate + 1], S.selm)])

    V.wait_ge(S.lst, 128)
    V.tensor_scalar(T.soff[:, :], T.sendl[:, :], 4.0, 0.0, mul, AluOpType.max).then_inc(S.sos, 1)

    def block(q, e=0):
        return N + groups[ci].index(q) if e else q

    def last_offsets():
        terms = [(T.plc, 1.0, float(shift[0]), mul, add), (T.ofl, float(NS), None, mul)]
        terms += [(T.plc, float(CAPP * s), float(shift[s] - shift[s - 1]), AluOpType.is_ge, mul) for s in steps]
        terms += [(T.ofl, float(q), T.selk[:, q:q + 1], AluOpType.is_equal, mul) for q in groups[ci] if both]
        V.wait_ge(S.pl, 32)
        for i, (src, *a) in enumerate(terms):
            if both and i == nt - 2:
                q = groups[ci][0]
                once("V", "sbs", 1)
                V.tensor_scalar(T.selk[:, q:q + 2], T.selb[0:16, q:q + 2], NS * (block(q, 1) - q) / 512.0, None, mul).then_inc(S.sks, 1)
                V.wait_ge(S.sks, 1)
            V.tensor_scalar(T.terms[:, i:32 * nt:nt], src[:, :], *a).then_inc(S.trm, 1)

    def last_sums():
        V.wait_ge(S.trm, nt)
        V.wait_ge(S.kp1, 1)
        V.tensor_tensor_scan(T.sums[:, 0:32 * nt], T.keep[:, 0:32 * nt], T.terms[:, 0:32 * nt], 0.0, mul, add).then_inc(S.scn, 1)
        V.wait_ge(S.scn, 1)
        V.tensor_copy(T.pu[:, :], T.sums[:, nt - 1:32 * nt:nt]).then_inc(S.pus, 1)
        Y.wait_ge(S.pus, 1)
        for k in range(8):
            Y.dma_start(T.poff[16 * k:16 * k + 16, :], T.pu[:, :]).then_inc(S.pr, 16)

    vec, act = PLAN["vec"].split(), PLAN["act"].split()

    def copy(q, out, src, sem):
        if q == "V":
            V.tensor_copy(out, src).then_inc(sem, 1)
        else:
            A.activation(out, src, Copy).then_inc(sem, 1)

    def gather(q, name):
        tile, part = name.split(".")
        sem = S[tile + "_" + q.lower()]
        if tile[0] == "t":
            once(q, "sos", 1)
            once(q, "xl", 16)
            t, d = int(part), groups[(ci + int(tile[1])) % C][0]
            copy(q, T[tile + "_g"][:, t:4 * PAIR:4], T.xs[:, t:4 * TK].indirect(T.soff[:, 6 * d:6 * d + 12]), sem)
        else:
            once(q, "wl", 32)
            once(q, tile + "_o", 2)
            l0, l1 = (0, PLAN["share"][tile]) if q == "A" else (PLAN["share"][tile], 64)
            copy(q, T[tile + "_g"][:, 16 * l0:16 * l1], T.ws[:, :].indirect(T[tile + "_o"][:, l0:l1]), sem)

    def quantise(tile):
        for names, s in ((vec, "_v"), (act, "_a")):
            n = len([a for a in names if a.startswith(tile + ".")])
            if n:
                V.wait_ge(S[tile + s], n)
        if tile == "t0":
            c = (NS - CAPP) * (1 - mine)
            V.quantize_mx(T.r_c[:, c:c + PAIR], T.r_s[:, c:c + PAIR], T.t0_g[:, :]).then_inc(S.t0_q, 1)
        else:
            V.quantize_mx(T[tile + "_c"][:, :], T[tile + "_s"][:, :], T[tile + "_g"][:, :]).then_inc(S[tile + "_q"], 1)

    def offsets(tile):
        once("V", "lns", 1)
        for i, part in enumerate(PLAN["tiles"][tile]):
            d, k = _peer(groups, r, part, 1), int(part[0])
            if d == r:
                once("V", "sbs", 1)
            elif d == mate:
                once("V", "selm", len(ups))
            else:
                once("V", "sel%d" % [ks[0] for way in "DB" for ks in PLAN["sel"][way] if k in ks][0], len(eng))
            V.tensor_scalar(T[tile + "_o"][:, 32 * i:32 * i + 32], T.lin[:, :], (T.selb if d == r else T.sland)[:, d:d + 1], None,
                            add).then_inc(S[tile + "_o"], 1)

    for name in vec:
        if name == "T":
            last_offsets()
        elif name == "S":
            last_sums()
        elif name == "w":
            once("V", "wl", 32)
            V.quantize_mx(T.w_c[:, :], T.w_s[:, :], T.ws[:, :]).then_inc(S.w_q, 1)
        elif name[0] == "o":
            offsets("e" + name[1])
        elif "." in name:
            gather("V", name)
        else:
            quantise(name)
    for name in act:
        gather("A", name)

    for tile in PLAN["send"].split():
        g.wait_ge(S[tile + "_q"], 1)
        if tile == "t0":
            chip_write(cores[mate], "r_", _slot_col(groups, mate, r), "r_", NS * (1 - mine), CAPP, ["tok0", "tok0"])
        elif tile == "w":
            chip_write(cores[mate], "m_", 0, "w_", 0, 256, ["me", "me"])
        elif tile == "ed":
            chip_write(cores[mate], "a_", 128 * r, "ed_", 0, 128, ["ex%d" % r] * 2)
        else:
            relayed = [_source(groups, r, tile, i) for i, w in enumerate(PLAN["way"][tile]) if w == "B"]
            if relayed:
                c = min(c for n, c in relayed)
                chip_write(rel, tile + "_", c, tile + "_", c, sum(n for n, c in relayed), [tile + "_c", tile + "_s"])
            _out(g, T, topo, groups, sent, eng, r, tile, "DM")

    def expert(name):
        if name[0] == "w":
            return block(r, int(name[1])), "w_", 128 * int(name[1]), "w_q", 1
        if name[0] == "m":
            return block(mate, int(name[1])), "m_", 128 * int(name[1]), "me", 2 * len(ups)
        if name == "00":
            return r, "ed_", 128, "ed_q", 1
        q = _peer(groups, r, name, -1)
        if q == mate:
            return q, "a_", 128 * q, "ex%d" % q, 2 * len(ups)
        tile = [t for t in PLAN["way"] if t[0] == "e" and name in PLAN["tiles"][t]][0]
        return q, "a_", 128 * q, "ex%d" % q, _landed(tile, PLAN["tiles"][tile].index(name), eng)

    units = [u.split(".") for u in PLAN["units"].split()]
    load = {"V": PLAN["ahead"], "A": 0}
    for u, (name, piece) in enumerate(units):
        blk, buf, col, sem, cnt = expert(name)
        once("T", sem, cnt)
        c0, c1 = PLAN["cut"][piece]
        for k in PLAN["lay"][c0 // PAIR:(c1 - 1) // PAIR + 1]:
            if k == 0:
                once("T", "t0_q", 1)
            once("T", "tok%d" % k, sum(_landed("t%d" % k, i, eng) for i in range(2)) if k else 2 * len(ups))
        if u >= 8:
            Te.wait_ge(S["ev%d" % (u - 8)], 1)
        p0, n = c0 if mine else NS - c1, c1 - c0
        b0, c0 = 512 * (u % 8), p0 + CAPP * mine
        Te.matmul_mx(T.ps[:, b0:b0 + n], T[buf + "c"][:, col:col + 128], T[buf + "s"][:, col:col + 128],
                     T.r_c[:, c0:c0 + n], T.r_s[:, c0:c0 + n], True, True).then_inc(S["mm%d" % u], 1)
        q = "V" if load["V"] <= load["A"] else "A"
        load[q] += n + 64
        queue[q].wait_ge(S["mm%d" % u], 1)
        copy(q, T.pw[:, NS * blk + p0:NS * blk + p0 + n], T.ps[:, b0:b0 + n], S["ev%d" % u] if u < len(units) - 8 else S.evz)

    pw = T.pw[:, 0:(N + 2 * both) * NS]
    for E in (V, A):
        E.wait_ge(S.pr, 128)
        E.wait_ge(S.evz, 8)
    n = TK // PLAN["stores"]
    for i in range(PLAN["stores"]):
        copy("VA"[i % 2], T.yb[:, n * i:n * i + n], pw.indirect(T.poff[:, n * i // 16:(n * i + n) // 16]), S["yg%d" % i])
    for i in range(PLAN["stores"]):
        E = A if i == PLAN["stores"] - 1 else Y
        E.wait_ge(S["yg%d" % i], 1)
        E.dma_start(T.y[:, n * i:n * i + n], T.yb[:, n * i:n * i + n]).then_inc(S.ys, 16)
    Y.wait_ge(S.ys, 16 * PLAN["stores"])
    g.wait_ge(S.sent, sent[0])
